import numpy as np
import ml_dtypes


def mxq(x, axis, fmt="e4m3"):
    dtype, down = {"e4m3": (ml_dtypes.float8_e4m3fn, 7), "e5m2": (ml_dtypes.float8_e5m2, 14)}[fmt]
    v = np.moveaxis(np.asarray(x, np.float32).astype(ml_dtypes.bfloat16).astype(np.float64), axis, -1)
    blocks = v.reshape(v.shape[:-1] + (-1, 32))
    amax = np.abs(blocks).max(-1, keepdims=True)
    byte = np.maximum(np.where(amax > 0, np.frexp(amax)[1] - 1 + 127, 0) - down, 1)
    scale = np.exp2(byte - 127.0)
    codes = (blocks / scale).astype(np.float32).astype(dtype).astype(np.float64)
    return np.moveaxis((codes * scale).reshape(v.shape), -1, axis)


WIDE = False


def mx_kscale(k):
    if not WIDE:
        return np.ones(k)
    levels = np.array([10, -10, 5, -5, 0])
    if k % 512:
        return np.exp2(np.random.permutation(np.resize(levels, k // 32))).repeat(32)
    a = np.empty((k // 512, 16))
    for p in range(k // 512):
        a[p, :8] = np.random.permutation(np.resize(levels, 8))
        for g in range(8):
            far = levels[np.abs(levels - a[p, g]) >= 10]
            a[p, g + 8] = far[np.random.randint(len(far))]
    return np.exp2(a.ravel()).repeat(32)


def f64(x):
    return np.asarray(x).astype(np.float64)


def striped(idx):
    return np.tile(idx.reshape(-1, 16).T, (8, 1)).astype(np.uint16)


def unstriped(offs):
    return offs[:16].T.reshape(-1).astype(np.int64)


def pack_weight(w):
    k, n = w.shape
    w = f64(np.asarray(w, np.float32).astype(ml_dtypes.bfloat16)).reshape(k // 32, 32, n)
    amax = np.abs(w).max(1)
    byte = np.clip(np.where(amax > 0, np.frexp(amax)[1] - 1 + 127 - 7, 1), 1, 254)
    scaled = (w * np.exp2(127.0 - byte)[:, None, :]).reshape(k, n).astype(np.float32)
    words = np.ascontiguousarray(scaled.reshape(k // 512, 128, 4, n).transpose(0, 1, 3, 2)).astype(ml_dtypes.float8_e4m3fn).view(np.uint8)
    return words, np.ascontiguousarray(byte.astype(np.uint8).reshape(k // 512, 16, n))


def unpack_weight(words, scales):
    g, p, n, _ = words.shape
    vals = np.ascontiguousarray(words).view(ml_dtypes.float8_e4m3fn).astype(np.float64) * np.repeat(np.exp2(scales.astype(np.float64) - 127.0), 8, axis=1)[..., None]
    return vals.transpose(0, 1, 3, 2).reshape(g * 512, n)


K, T, S, J = 1024, 2048, 512, 512
P = 2 ** 7


def setup_inputs():
    n = np.random.standard_normal
    s = mx_kscale(K)[:, None]
    packed_xT = pack_weight(n((K, T)) * s)
    return {
        "x_words": packed_xT[0],
        "x_scales": packed_xT[1],
        "hT": (n((K, J)) / np.sqrt(K) / s).astype(np.float32),
        "inv": (np.tile(np.random.uniform(0.5, 1.5, T), (P, 1))).astype(np.float32),
        "offs": striped(np.random.permutation(T)[:S]),
    }


def reference(x_words, x_scales, hT, inv, offs):
    hTq = mxq(f64(hT), 0, "e4m3")
    xq = unpack_weight(x_words, x_scales)[:, unstriped(offs)]
    y = (hTq.T @ xq) * (f64(inv)[:1][:, unstriped(offs)])
    l = 4.0 * y
    e = np.exp(l - l.max(axis=1, keepdims=True))
    return e / e.sum(axis=1, keepdims=True)

@@ -1,0 +1,144 @@
+from contextlib import ExitStack
+
+import concourse.mybir as mybir
+from concourse.masks import make_identity
+
+K, T, S, J = 1024, 2048, 512, 512
+P = 128
+PACK = 4
+PASSES = K // (P * PACK)
+BLOCKS = J // P
+FLOPS = 2 * K * S * J
+
+F32 = mybir.dt.float32
+BF16 = mybir.dt.bfloat16
+I32 = mybir.dt.int32
+U32 = mybir.dt.uint32
+U16 = mybir.dt.uint16
+U8 = mybir.dt.uint8
+FP8X4 = mybir.dt.float8_e4m3fn_x4
+ALU = mybir.AluOpType
+ACT = mybir.ActivationFunctionType
+
+
+def tile_picked_zcos_soft_p_kernel(tc, x_words, x_scales, hT, inv, offs, out):
+    nc = tc.nc
+    with ExitStack() as ctx:
+        keep = ctx.enter_context(tc.tile_pool(name="keep", bufs=1))
+        psum = ctx.enter_context(tc.psum_pool(name="psum", bufs=1))
+
+        offsets = keep.tile([P, S // 16], U16, name="offsets")
+        nc.sync.dma_start(offsets[:], offs)
+
+        planes = keep.tile([P, T], U8, name="planes", align_bytes=64)
+        nc.vector.memset(planes[:].bitcast(I32), 0)
+        for q in range(4):
+            nc.scalar.dma_start(
+                out=planes[32 * q : 32 * q + 4 * PASSES, :].bitcast(I32),
+                in_=x_scales[:, 4 * q : 4 * q + 4, :].bitcast(I32),
+            )
+        inv_row = keep.tile([P, T], F32, name="inv_row")
+        nc.vector.memset(inv_row[:], 0.0)
+        nc.scalar.dma_start(out=inv_row[0:1, :], in_=inv[0:1, :])
+
+        warm_in = keep.tile([P, 1], F32, name="warm_in")
+        warm_out = keep.tile([P, 1], F32, name="warm_out")
+        nc.vector.memset(warm_in[:], 0.0)
+        nc.scalar.activation(out=warm_out[:], in_=warm_in[:], func=ACT.Exp)
+
+        ident = keep.tile([P, P], F32, name="ident")
+        make_identity(nc, ident[:])
+
+        tables = [keep.tile([P, T], I32, name=f"table{o}") for o in range(PASSES)]
+        raws = [[keep.tile([P, PACK, P], F32, name=f"raw{b}_{o}") for o in range(PASSES)] for b in range(BLOCKS)]
+
+        def load_table(o):
+            nc.sync.dma_start(out=tables[o][:], in_=x_words[o].rearrange("p n t -> p (n t)").bitcast(I32))
+
+        def load_queries(b, o):
+            rows = hT[o * P * PACK : (o + 1) * P * PACK, b * P : (b + 1) * P]
+            nc.sync.dma_start(out=raws[b][o][:], in_=rows.rearrange("(p j) w -> p j w", j=PACK))
+
+        load_table(0)
+        load_queries(0, 0)
+        load_queries(0, 1)
+        load_table(1)
+        for b in range(1, BLOCKS):
+            for o in range(PASSES):
+                load_queries(b, o)
+
+        x_planes = keep.tile([P, S], U8, name="x_planes", align_bytes=64)
+        nc.vector.tensor_copy(x_planes[:], planes[:].indirect(offsets[:]))
+        inv_picked = keep.tile([P, S], F32, name="inv_picked")
+        nc.vector.tensor_copy(inv_picked[:], inv_row[:].indirect(offsets[:]))
+
+        turned = psum.tile([P, BLOCKS, P], F32, name="turned")
+        for c in range(S // P):
+            nc.tensor.transpose(turned[:, c, :], inv_picked[:, c * P : (c + 1) * P], ident[:])
+        inv_cols = keep.tile([P, S // P], F32, name="inv_cols")
+        nc.scalar.activation(out=inv_cols[:], in_=turned[:, :, 0], func=ACT.Copy, scale=-4.0)
+        spread = psum.tile([P, S], F32, name="spread")
+        for c in range(S // P):
+            nc.tensor.transpose(spread[:, c * P : (c + 1) * P], inv_cols[:, c : c + 1].to_broadcast([P, P]), ident[:])
+        factor = keep.tile([P, S], F32, name="factor")
+        nc.scalar.copy(out=factor[:], in_=spread[:])
+
+        x_codes = [keep.tile([P, S], U32, name=f"x_codes{o}", align_bytes=64) for o in range(PASSES)]
+        logits = [psum.tile([P, S], F32, name=f"logits{b}") for b in range(BLOCKS)]
+
+        def gather_codes(o):
+            nc.vector.tensor_copy(x_codes[o][:], tables[o][:].bitcast(U32).indirect(offsets[:]))
+
+        quantised = {}
+
+        def quantise(b, o):
+            grouped = keep.tile([P, P, PACK], BF16, name=f"grouped{b}_{o}", align_bytes=64)
+            nc.scalar.copy(
+                out=grouped[:].rearrange("p (c i) t -> p c t i", i=4),
+                in_=raws[b][o][:].rearrange("p t (c i) -> p c t i", i=4),
+            )
+            codes = keep.tile([P, P], U32, name=f"h_codes{b}_{o}", align_bytes=64)
+            scales = keep.tile([P, P], U8, name=f"h_scales{b}_{o}", align_bytes=64)
+            nc.vector.quantize_mx(
+                out=codes[:].bitcast(FP8X4), scales=scales[:], in_=grouped[:].rearrange("p w j -> p (w j)")
+            )
+            quantised[(b, o)] = (codes, scales)
+
+        def product(b, o):
+            codes, scales = quantised[(b, o)]
+            nc.tensor.matmul_mx(
+                out=logits[b][:],
+                lhsT=codes[:].bitcast(FP8X4),
+                lhsT_scale=scales[:],
+                rhs=x_codes[o][:].bitcast(FP8X4),
+                rhs_scale=x_planes[4 * o : P, :],
+                start=(o == 0),
+                stop=(o == PASSES - 1),
+            )
+
+        def softmax(b):
+            negl = keep.tile([P, S], F32, name=f"negl{b}")
+            nc.vector.tensor_tensor(negl[:], logits[b][:], factor[:], ALU.mult)
+            least = keep.tile([P, 1], F32, name=f"least{b}")
+            nc.vector.tensor_reduce(least[:], negl[:], mybir.AxisListType.X, ALU.min)
+            expd = keep.tile([P, S], F32, name=f"expd{b}")
+            total = keep.tile([P, 1], F32, name=f"total{b}")
+            nc.scalar.activation(out=expd[:], in_=negl[:], func=ACT.Exp, bias=least[:], scale=-1.0, accum_out=total[:])
+            share = keep.tile([P, 1], F32, name=f"share{b}")
+            nc.vector.reciprocal(share[:], total[:])
+            weights = keep.tile([P, S], F32, name=f"weights{b}")
+            nc.vector.tensor_scalar(weights[:], expd[:], share[:], None, ALU.mult)
+            nc.sync.dma_start(out=out[b * P : (b + 1) * P, :], in_=weights[:])
+
+        gather_codes(0)
+        quantise(0, 0)
+        quantise(0, 1)
+        product(0, 0)
+        gather_codes(1)
+        product(0, 1)
+        for b in range(1, BLOCKS):
+            for o in range(PASSES):
+                quantise(b, o)
+                product(b, o)
+            softmax(b - 1)
+        softmax(BLOCKS - 1)

@@ -20,46 +20,63 @@ FP8X4 = mybir.dt.float8_e4m3fn_x4
 ALU = mybir.AluOpType
 ACT = mybir.ActivationFunctionType
 
+KB = 1024
+INV_AT = 2 * KB
+PLANES_AT = 42 * KB
+TABLE_AT = {0: 10 * KB, 1: 18 * KB}
+XCODES_AT = {0: 26 * KB, 1: 1 * KB}
+RAW_AT = {(b, o): (44 + 4 * b + 2 * o) * KB for b in range(BLOCKS) for o in range(PASSES)}
+GROUPED_AT = {(0, 0): 0, (0, 1): KB, (1, 0): 3 * KB, (1, 1): 4 * KB, (2, 0): 5 * KB, (2, 1): 6 * KB, (3, 0): 7 * KB, (3, 1): 8 * KB}
+CODES_AT = {(b, o): (TABLE_AT[1] if b else PLANES_AT) + (2 * b + o) * 512 for b in range(BLOCKS) for o in range(PASSES)}
+SCALES_AT = {(b, o): (36 if b else 38) * KB + o * KB for b in range(BLOCKS) for o in range(PASSES)}
+HALF = S // 2
+
 
 def tile_picked_zcos_soft_p_kernel(tc, x_words, x_scales, hT, inv, offs, out):
     nc = tc.nc
     with ExitStack() as ctx:
         keep = ctx.enter_context(tc.tile_pool(name="keep", bufs=1))
+        reuse = ctx.enter_context(tc.tile_pool(name="reuse", bufs=1))
         psum = ctx.enter_context(tc.psum_pool(name="psum", bufs=1))
 
         offsets = keep.tile([P, S // 16], U16, name="offsets")
-        nc.sync.dma_start(offsets[:], offs)
 
-        planes = keep.tile([P, T], U8, name="planes", align_bytes=64)
-        nc.vector.memset(planes[:].bitcast(I32), 0)
-        for q in range(4):
-            nc.scalar.dma_start(
-                out=planes[32 * q : 32 * q + 4 * PASSES, :].bitcast(I32),
-                in_=x_scales[:, 4 * q : 4 * q + 4, :].bitcast(I32),
-            )
-        inv_row = keep.tile([P, T], F32, name="inv_row")
-        nc.vector.memset(inv_row[:], 0.0)
-        nc.scalar.dma_start(out=inv_row[0:1, :], in_=inv[0:1, :])
+        planes = reuse.tile([P, T], U8, name="planes", align_bytes=64, offset=PLANES_AT)
+        inv_cols = reuse.tile([P, T // P], F32, name="inv_cols", offset=KB - 32)
+        nc.scalar.dma_start(out=inv_cols[:], in_=inv[0, :].rearrange("(p i) -> p i", p=P))
 
         warm_in = keep.tile([P, 1], F32, name="warm_in")
         warm_out = keep.tile([P, 1], F32, name="warm_out")
         nc.vector.memset(warm_in[:], 0.0)
+        nc.vector.memset(planes[:].bitcast(I32), 0)
         nc.scalar.activation(out=warm_out[:], in_=warm_in[:], func=ACT.Exp)
 
         ident = keep.tile([P, P], F32, name="ident")
         make_identity(nc, ident[:])
 
-        tables = [keep.tile([P, T], I32, name=f"table{o}") for o in range(PASSES)]
-        raws = [[keep.tile([P, PACK, P], F32, name=f"raw{b}_{o}") for o in range(PASSES)] for b in range(BLOCKS)]
+        for q in range(4):
+            nc.gpsimd.dma_start(
+                out=planes[32 * q : 32 * q + 4 * PASSES, :].bitcast(I32),
+                in_=x_scales[:, 4 * q : 4 * q + 4, :].bitcast(I32),
+            )
+        minus_one = keep.tile([P, 1], F32, name="minus_one")
+        nc.gpsimd.memset(minus_one[:], -1.0)
+
+        tables = [
+            reuse.tile([P, T], I32, name=f"table{o}", align_bytes=64, offset=TABLE_AT[o]) for o in range(PASSES)
+        ]
+        raws = {}
 
         def load_table(o):
             nc.sync.dma_start(out=tables[o][:], in_=x_words[o].rearrange("p n t -> p (n t)").bitcast(I32))
 
         def load_queries(b, o):
             rows = hT[o * P * PACK : (o + 1) * P * PACK, b * P : (b + 1) * P]
-            nc.sync.dma_start(out=raws[b][o][:], in_=rows.rearrange("(p j) w -> p j w", j=PACK))
+            raws[(b, o)] = reuse.tile([P, PACK, P], F32, name=f"raw{b}_{o}", align_bytes=64, offset=RAW_AT[(b, o)])
+            nc.sync.dma_start(out=raws[(b, o)][:], in_=rows.rearrange("(p j) w -> p j w", j=PACK))
 
         load_table(0)
+        nc.sync.dma_start(offsets[:], offs)
         load_queries(0, 0)
         load_queries(0, 1)
         load_table(1)
@@ -67,78 +84,129 @@ def tile_picked_zcos_soft_p_kernel(tc, x_words, x_scales, hT, inv, offs, out):
             for o in range(PASSES):
                 load_queries(b, o)
 
+        inv_rows = reuse.tile([P, T], F32, name="inv_rows", align_bytes=64, offset=INV_AT)
+        for g in range(4):
+            spread = psum.tile([P, 4, P], F32, name=f"spread{g}", tag=f"bank{g}")
+            for i in range(4):
+                column = inv_cols[:, 4 * g + i : 4 * g + i + 1]
+                nc.tensor.transpose(spread[:, i, :], column.to_broadcast([P, P]), ident[:])
+            nc.scalar.copy(
+                out=inv_rows[:].rearrange("p (n g i) -> p g n i", g=4, i=4)[:, g],
+                in_=spread[:].rearrange("p i n -> p n i"),
+            )
+
         x_planes = keep.tile([P, S], U8, name="x_planes", align_bytes=64)
-        nc.vector.tensor_copy(x_planes[:], planes[:].indirect(offsets[:]))
-        inv_picked = keep.tile([P, S], F32, name="inv_picked")
-        nc.vector.tensor_copy(inv_picked[:], inv_row[:].indirect(offsets[:]))
-
-        turned = psum.tile([P, BLOCKS, P], F32, name="turned")
-        for c in range(S // P):
-            nc.tensor.transpose(turned[:, c, :], inv_picked[:, c * P : (c + 1) * P], ident[:])
-        inv_cols = keep.tile([P, S // P], F32, name="inv_cols")
-        nc.scalar.activation(out=inv_cols[:], in_=turned[:, :, 0], func=ACT.Copy, scale=-4.0)
-        spread = psum.tile([P, S], F32, name="spread")
-        for c in range(S // P):
-            nc.tensor.transpose(spread[:, c * P : (c + 1) * P], inv_cols[:, c : c + 1].to_broadcast([P, P]), ident[:])
         factor = keep.tile([P, S], F32, name="factor")
-        nc.scalar.copy(out=factor[:], in_=spread[:])
 
-        x_codes = [keep.tile([P, S], U32, name=f"x_codes{o}", align_bytes=64) for o in range(PASSES)]
-        logits = [psum.tile([P, S], F32, name=f"logits{b}") for b in range(BLOCKS)]
+        x_codes = {}
+        logits = {}
 
-        def gather_codes(o):
-            nc.vector.tensor_copy(x_codes[o][:], tables[o][:].bitcast(U32).indirect(offsets[:]))
+        def gather_codes(o, parts):
+            x_codes[o] = reuse.tile([P, S], U32, name=f"x_codes{o}", align_bytes=64, offset=XCODES_AT[o])
+            for lo, hi in parts:
+                nc.vector.tensor_copy(
+                    x_codes[o][:, lo:hi], tables[o][:].bitcast(U32).indirect(offsets[:, lo // 16 : hi // 16])
+                )
+
+        whole = [(0, S)]
+        halves = [(0, HALF), (HALF, S)]
 
         quantised = {}
 
-        def quantise(b, o):
-            grouped = keep.tile([P, P, PACK], BF16, name=f"grouped{b}_{o}", align_bytes=64)
+        groups = {}
+
+        def interleave(b, o):
+            grouped = reuse.tile([P, P, PACK], BF16, name=f"grouped{b}_{o}", align_bytes=64, offset=GROUPED_AT[(b, o)])
             nc.scalar.copy(
                 out=grouped[:].rearrange("p (c i) t -> p c t i", i=4),
-                in_=raws[b][o][:].rearrange("p t (c i) -> p c t i", i=4),
+                in_=raws[(b, o)][:].rearrange("p t (c i) -> p c t i", i=4),
             )
-            codes = keep.tile([P, P], U32, name=f"h_codes{b}_{o}", align_bytes=64)
-            scales = keep.tile([P, P], U8, name=f"h_scales{b}_{o}", align_bytes=64)
+            groups[(b, o)] = grouped
+
+        def quantise(b, o):
+            grouped = groups[(b, o)]
+            codes = reuse.tile([P, P], U32, name=f"h_codes{b}_{o}", align_bytes=64, offset=CODES_AT[(b, o)])
+            scales = reuse.tile([P, P], U8, name=f"h_scales{b}_{o}", align_bytes=64, offset=SCALES_AT[(b, o)])
             nc.vector.quantize_mx(
                 out=codes[:].bitcast(FP8X4), scales=scales[:], in_=grouped[:].rearrange("p w j -> p (w j)")
             )
             quantised[(b, o)] = (codes, scales)
 
-        def product(b, o):
+        def product(b, o, parts):
             codes, scales = quantised[(b, o)]
-            nc.tensor.matmul_mx(
-                out=logits[b][:],
-                lhsT=codes[:].bitcast(FP8X4),
-                lhsT_scale=scales[:],
-                rhs=x_codes[o][:].bitcast(FP8X4),
-                rhs_scale=x_planes[4 * o : P, :],
-                start=(o == 0),
-                stop=(o == PASSES - 1),
+            for lo, hi in parts:
+                if o == 0:
+                    logits[(b, lo)] = psum.tile([P, hi - lo], F32, name=f"logits{b}_{lo}", tag=f"bank{4 + b if lo == 0 else 0}")
+                nc.tensor.matmul_mx(
+                    out=logits[(b, lo)][:],
+                    lhsT=codes[:].bitcast(FP8X4),
+                    lhsT_scale=scales[:],
+                    rhs=x_codes[o][:, lo:hi].bitcast(FP8X4),
+                    rhs_scale=x_planes[4 * o : P, lo:hi],
+                    start=(o == 0),
+                    stop=(o == PASSES - 1),
+                )
+
+        negls = [keep.tile([P, S], F32, name=f"negl{b}") for b in range(BLOCKS)]
+
+        def scale(b, lo, hi):
+            nc.vector.scalar_tensor_tensor(
+                negls[b][:, lo:hi], logits[(b, lo)][:], -4.0, factor[:, lo:hi], ALU.mult, ALU.mult
             )
 
+        expds = {}
+
         def softmax(b):
-            negl = keep.tile([P, S], F32, name=f"negl{b}")
-            nc.vector.tensor_tensor(negl[:], logits[b][:], factor[:], ALU.mult)
+            negl = negls[b]
             least = keep.tile([P, 1], F32, name=f"least{b}")
             nc.vector.tensor_reduce(least[:], negl[:], mybir.AxisListType.X, ALU.min)
             expd = keep.tile([P, S], F32, name=f"expd{b}")
             total = keep.tile([P, 1], F32, name=f"total{b}")
             nc.scalar.activation(out=expd[:], in_=negl[:], func=ACT.Exp, bias=least[:], scale=-1.0, accum_out=total[:])
+            expds[b] = (expd, total)
+
+        def normalise(b):
+            expd, total = expds[b]
             share = keep.tile([P, 1], F32, name=f"share{b}")
-            nc.vector.reciprocal(share[:], total[:])
             weights = keep.tile([P, S], F32, name=f"weights{b}")
-            nc.vector.tensor_scalar(weights[:], expd[:], share[:], None, ALU.mult)
+            if b >= BLOCKS - 2:
+                nc.vector.reciprocal(share[:], total[:])
+                nc.vector.tensor_scalar(weights[:], expd[:], share[:], None, ALU.mult)
+            else:
+                nc.gpsimd.tensor_tensor(share[:], total[:], minus_one[:], ALU.pow)
+                nc.gpsimd.tensor_scalar(weights[:], expd[:], share[:], 0.0, ALU.mult, ALU.add)
             nc.sync.dma_start(out=out[b * P : (b + 1) * P, :], in_=weights[:])
 
-        gather_codes(0)
-        quantise(0, 0)
-        quantise(0, 1)
-        product(0, 0)
-        gather_codes(1)
-        product(0, 1)
+        def feed(b, o):
+            quantise(b, o)
+            product(b, o, whole)
+
+        gather_codes(0, whole)
+        nc.vector.tensor_copy(factor[:], inv_rows[:].indirect(offsets[:]))
+        nc.vector.tensor_copy(x_planes[:], planes[:].indirect(offsets[:]))
+        for o in range(PASSES):
+            interleave(0, o)
+            quantise(0, o)
+        product(0, 0, halves)
+        gather_codes(1, halves)
+        product(0, 1, halves)
         for b in range(1, BLOCKS):
             for o in range(PASSES):
-                quantise(b, o)
-                product(b, o)
-            softmax(b - 1)
-        softmax(BLOCKS - 1)
+                interleave(b, o)
+        scale(0, 0, HALF)
+        feed(1, 0)
+        scale(0, HALF, S)
+        feed(1, 1)
+        softmax(0)
+        feed(2, 0)
+        scale(1, 0, S)
+        feed(2, 1)
+        softmax(1)
+        feed(3, 0)
+        feed(3, 1)
+        scale(2, 0, S)
+        softmax(2)
+        scale(3, 0, S)
+        softmax(3)
+        for b in range(BLOCKS):
+            normalise(b)

@@ -43,22 +43,17 @@ def tile_picked_zcos_soft_p_kernel(tc, x_words, x_scales, hT, inv, offs, out):
 
         planes = reuse.tile([P, T], U8, name="planes", align_bytes=64, offset=PLANES_AT)
         inv_cols = reuse.tile([P, T // P], F32, name="inv_cols", offset=KB - 32)
-        nc.scalar.dma_start(out=inv_cols[:], in_=inv[0, :].rearrange("(p i) -> p i", p=P))
+        nc.sync.dma_start(out=inv_cols[:], in_=inv[0, :].rearrange("(p i) -> p i", p=P))
 
+        nc.gpsimd.memset(planes[:].bitcast(I32), 0)
         warm_in = keep.tile([P, 1], F32, name="warm_in")
         warm_out = keep.tile([P, 1], F32, name="warm_out")
         nc.vector.memset(warm_in[:], 0.0)
-        nc.vector.memset(planes[:].bitcast(I32), 0)
         nc.scalar.activation(out=warm_out[:], in_=warm_in[:], func=ACT.Exp)
 
         ident = keep.tile([P, P], F32, name="ident")
         make_identity(nc, ident[:])
 
-        for q in range(4):
-            nc.gpsimd.dma_start(
-                out=planes[32 * q : 32 * q + 4 * PASSES, :].bitcast(I32),
-                in_=x_scales[:, 4 * q : 4 * q + 4, :].bitcast(I32),
-            )
         minus_one = keep.tile([P, 1], F32, name="minus_one")
         nc.gpsimd.memset(minus_one[:], -1.0)
 
@@ -77,6 +72,11 @@ def tile_picked_zcos_soft_p_kernel(tc, x_words, x_scales, hT, inv, offs, out):
 
         load_table(0)
         nc.sync.dma_start(offsets[:], offs)
+        for q in range(4):
+            nc.sync.dma_start(
+                out=planes[32 * q : 32 * q + 4 * PASSES, :].bitcast(I32),
+                in_=x_scales[:, 4 * q : 4 * q + 4, :].bitcast(I32),
+            )
         load_queries(0, 0)
         load_queries(0, 1)
         load_table(1)
@@ -169,21 +169,26 @@ def tile_picked_zcos_soft_p_kernel(tc, x_words, x_scales, hT, inv, offs, out):
             expd, total = expds[b]
             share = keep.tile([P, 1], F32, name=f"share{b}")
             weights = keep.tile([P, S], F32, name=f"weights{b}")
+            parts = halves if b == BLOCKS - 1 else whole
             if b >= BLOCKS - 2:
                 nc.vector.reciprocal(share[:], total[:])
-                nc.vector.tensor_scalar(weights[:], expd[:], share[:], None, ALU.mult)
             else:
                 nc.gpsimd.tensor_tensor(share[:], total[:], minus_one[:], ALU.pow)
-                nc.gpsimd.tensor_scalar(weights[:], expd[:], share[:], 0.0, ALU.mult, ALU.add)
-            nc.sync.dma_start(out=out[b * P : (b + 1) * P, :], in_=weights[:])
+            for lo, hi in parts:
+                if b >= BLOCKS - 2:
+                    nc.vector.tensor_scalar(weights[:, lo:hi], expd[:, lo:hi], share[:], None, ALU.mult)
+                else:
+                    nc.gpsimd.tensor_scalar(weights[:, lo:hi], expd[:, lo:hi], share[:], 0.0, ALU.mult, ALU.add)
+                queue = nc.scalar if lo else nc.sync
+                queue.dma_start(out=out[b * P : (b + 1) * P, lo:hi], in_=weights[:, lo:hi])
 
         def feed(b, o):
             quantise(b, o)
             product(b, o, whole)
 
         gather_codes(0, whole)
-        nc.vector.tensor_copy(factor[:], inv_rows[:].indirect(offsets[:]))
         nc.vector.tensor_copy(x_planes[:], planes[:].indirect(offsets[:]))
+        nc.vector.tensor_copy(factor[:], inv_rows[:].indirect(offsets[:]))
         for o in range(PASSES):
             interleave(0, o)
             quantise(0, o)
@@ -203,8 +208,8 @@ def tile_picked_zcos_soft_p_kernel(tc, x_words, x_scales, hT, inv, offs, out):
         feed(2, 1)
         softmax(1)
         feed(3, 0)
-        feed(3, 1)
         scale(2, 0, S)
+        feed(3, 1)
         softmax(2)
         scale(3, 0, S)
         softmax(3)

from contextlib import ExitStack

import concourse.mybir as mybir
from concourse.masks import make_identity

K, T, S, J = 1024, 2048, 512, 512
P = 128
PACK = 4
PASSES = K // (P * PACK)
BLOCKS = J // P
FLOPS = 2 * K * S * J

F32 = mybir.dt.float32
BF16 = mybir.dt.bfloat16
I32 = mybir.dt.int32
U32 = mybir.dt.uint32
U16 = mybir.dt.uint16
U8 = mybir.dt.uint8
FP8X4 = mybir.dt.float8_e4m3fn_x4
ALU = mybir.AluOpType
ACT = mybir.ActivationFunctionType

KB = 1024
INV_AT = 2 * KB
PLANES_AT = 42 * KB
TABLE_AT = {0: 10 * KB, 1: 18 * KB}
XCODES_AT = {0: 26 * KB, 1: 1 * KB}
RAW_AT = {(b, o): (44 + 4 * b + 2 * o) * KB for b in range(BLOCKS) for o in range(PASSES)}
GROUPED_AT = {(0, 0): 0, (0, 1): KB, (1, 0): 3 * KB, (1, 1): 4 * KB, (2, 0): 5 * KB, (2, 1): 6 * KB, (3, 0): 7 * KB, (3, 1): 8 * KB}
CODES_AT = {(b, o): (TABLE_AT[1] if b else PLANES_AT) + (2 * b + o) * 512 for b in range(BLOCKS) for o in range(PASSES)}
SCALES_AT = {(b, o): (36 if b else 38) * KB + o * KB for b in range(BLOCKS) for o in range(PASSES)}
HALF = S // 2


def tile_picked_zcos_soft_p_kernel(tc, x_words, x_scales, hT, inv, offs, out):
    nc = tc.nc
    with ExitStack() as ctx:
        keep = ctx.enter_context(tc.tile_pool(name="keep", bufs=1))
        reuse = ctx.enter_context(tc.tile_pool(name="reuse", bufs=1))
        psum = ctx.enter_context(tc.psum_pool(name="psum", bufs=1))

        offsets = keep.tile([P, S // 16], U16, name="offsets")

        planes = reuse.tile([P, T], U8, name="planes", align_bytes=64, offset=PLANES_AT)
        inv_cols = reuse.tile([P, T // P], F32, name="inv_cols", offset=KB - 32)
        nc.sync.dma_start(out=inv_cols[:], in_=inv[0, :].rearrange("(p i) -> p i", p=P))

        nc.gpsimd.memset(planes[:].bitcast(I32), 0)
        warm_in = keep.tile([P, 1], F32, name="warm_in")
        warm_out = keep.tile([P, 1], F32, name="warm_out")
        nc.vector.memset(warm_in[:], 0.0)
        nc.scalar.activation(out=warm_out[:], in_=warm_in[:], func=ACT.Exp)

        ident = keep.tile([P, P], F32, name="ident")
        make_identity(nc, ident[:])

        minus_one = keep.tile([P, 1], F32, name="minus_one")
        nc.gpsimd.memset(minus_one[:], -1.0)

        tables = [
            reuse.tile([P, T], I32, name=f"table{o}", align_bytes=64, offset=TABLE_AT[o]) for o in range(PASSES)
        ]
        raws = {}

        def load_table(o):
            nc.sync.dma_start(out=tables[o][:], in_=x_words[o].rearrange("p n t -> p (n t)").bitcast(I32))

        def load_queries(b, o):
            rows = hT[o * P * PACK : (o + 1) * P * PACK, b * P : (b + 1) * P]
            raws[(b, o)] = reuse.tile([P, PACK, P], F32, name=f"raw{b}_{o}", align_bytes=64, offset=RAW_AT[(b, o)])
            nc.sync.dma_start(out=raws[(b, o)][:], in_=rows.rearrange("(p j) w -> p j w", j=PACK))

        load_table(0)
        nc.sync.dma_start(offsets[:], offs)
        for q in range(4):
            nc.sync.dma_start(
                out=planes[32 * q : 32 * q + 4 * PASSES, :].bitcast(I32),
                in_=x_scales[:, 4 * q : 4 * q + 4, :].bitcast(I32),
            )
        load_queries(0, 0)
        load_queries(0, 1)
        load_table(1)
        for b in range(1, BLOCKS):
            for o in range(PASSES):
                load_queries(b, o)

        inv_rows = reuse.tile([P, T], F32, name="inv_rows", align_bytes=64, offset=INV_AT)
        for g in range(4):
            spread = psum.tile([P, 4, P], F32, name=f"spread{g}", tag=f"bank{g}")
            for i in range(4):
                column = inv_cols[:, 4 * g + i : 4 * g + i + 1]
                nc.tensor.transpose(spread[:, i, :], column.to_broadcast([P, P]), ident[:])
            nc.scalar.copy(
                out=inv_rows[:].rearrange("p (n g i) -> p g n i", g=4, i=4)[:, g],
                in_=spread[:].rearrange("p i n -> p n i"),
            )

        x_planes = keep.tile([P, S], U8, name="x_planes", align_bytes=64)
        factor = keep.tile([P, S], F32, name="factor")

        x_codes = {}
        logits = {}

        def gather_codes(o, parts):
            x_codes[o] = reuse.tile([P, S], U32, name=f"x_codes{o}", align_bytes=64, offset=XCODES_AT[o])
            for lo, hi in parts:
                nc.vector.tensor_copy(
                    x_codes[o][:, lo:hi], tables[o][:].bitcast(U32).indirect(offsets[:, lo // 16 : hi // 16])
                )

        whole = [(0, S)]
        halves = [(0, HALF), (HALF, S)]

        quantised = {}

        groups = {}

        def interleave(b, o):
            grouped = reuse.tile([P, P, PACK], BF16, name=f"grouped{b}_{o}", align_bytes=64, offset=GROUPED_AT[(b, o)])
            nc.scalar.copy(
                out=grouped[:].rearrange("p (c i) t -> p c t i", i=4),
                in_=raws[(b, o)][:].rearrange("p t (c i) -> p c t i", i=4),
            )
            groups[(b, o)] = grouped

        def quantise(b, o):
            grouped = groups[(b, o)]
            codes = reuse.tile([P, P], U32, name=f"h_codes{b}_{o}", align_bytes=64, offset=CODES_AT[(b, o)])
            scales = reuse.tile([P, P], U8, name=f"h_scales{b}_{o}", align_bytes=64, offset=SCALES_AT[(b, o)])
            nc.vector.quantize_mx(
                out=codes[:].bitcast(FP8X4), scales=scales[:], in_=grouped[:].rearrange("p w j -> p (w j)")
            )
            quantised[(b, o)] = (codes, scales)

        def product(b, o, parts):
            codes, scales = quantised[(b, o)]
            for lo, hi in parts:
                if o == 0:
                    logits[(b, lo)] = psum.tile([P, hi - lo], F32, name=f"logits{b}_{lo}", tag=f"bank{4 + b if lo == 0 else 0}")
                nc.tensor.matmul_mx(
                    out=logits[(b, lo)][:],
                    lhsT=codes[:].bitcast(FP8X4),
                    lhsT_scale=scales[:],
                    rhs=x_codes[o][:, lo:hi].bitcast(FP8X4),
                    rhs_scale=x_planes[4 * o : P, lo:hi],
                    start=(o == 0),
                    stop=(o == PASSES - 1),
                )

        negls = [keep.tile([P, S], F32, name=f"negl{b}") for b in range(BLOCKS)]

        def scale(b, lo, hi):
            nc.vector.scalar_tensor_tensor(
                negls[b][:, lo:hi], logits[(b, lo)][:], -4.0, factor[:, lo:hi], ALU.mult, ALU.mult
            )

        expds = {}

        def softmax(b):
            negl = negls[b]
            least = keep.tile([P, 1], F32, name=f"least{b}")
            nc.vector.tensor_reduce(least[:], negl[:], mybir.AxisListType.X, ALU.min)
            expd = keep.tile([P, S], F32, name=f"expd{b}")
            total = keep.tile([P, 1], F32, name=f"total{b}")
            nc.scalar.activation(out=expd[:], in_=negl[:], func=ACT.Exp, bias=least[:], scale=-1.0, accum_out=total[:])
            expds[b] = (expd, total)

        def normalise(b):
            expd, total = expds[b]
            share = keep.tile([P, 1], F32, name=f"share{b}")
            weights = keep.tile([P, S], F32, name=f"weights{b}")
            parts = halves if b == BLOCKS - 1 else whole
            if b >= BLOCKS - 2:
                nc.vector.reciprocal(share[:], total[:])
            else:
                nc.gpsimd.tensor_tensor(share[:], total[:], minus_one[:], ALU.pow)
            for lo, hi in parts:
                if b >= BLOCKS - 2:
                    nc.vector.tensor_scalar(weights[:, lo:hi], expd[:, lo:hi], share[:], None, ALU.mult)
                else:
                    nc.gpsimd.tensor_scalar(weights[:, lo:hi], expd[:, lo:hi], share[:], 0.0, ALU.mult, ALU.add)
                queue = nc.scalar if lo else nc.sync
                queue.dma_start(out=out[b * P : (b + 1) * P, lo:hi], in_=weights[:, lo:hi])

        def feed(b, o):
            quantise(b, o)
            product(b, o, whole)

        gather_codes(0, whole)
        nc.vector.tensor_copy(x_planes[:], planes[:].indirect(offsets[:]))
        nc.vector.tensor_copy(factor[:], inv_rows[:].indirect(offsets[:]))
        for o in range(PASSES):
            interleave(0, o)
            quantise(0, o)
        product(0, 0, halves)
        gather_codes(1, halves)
        product(0, 1, halves)
        for b in range(1, BLOCKS):
            for o in range(PASSES):
                interleave(b, o)
        scale(0, 0, HALF)
        feed(1, 0)
        scale(0, HALF, S)
        feed(1, 1)
        softmax(0)
        feed(2, 0)
        scale(1, 0, S)
        feed(2, 1)
        softmax(1)
        feed(3, 0)
        scale(2, 0, S)
        feed(3, 1)
        softmax(2)
        scale(3, 0, S)
        softmax(3)
        for b in range(BLOCKS):
            normalise(b)
